import numpy as np
import ml_dtypes


def mxq(x, axis, fmt="e4m3"):
    dtype, down = {"e4m3": (ml_dtypes.float8_e4m3fn, 7), "e5m2": (ml_dtypes.float8_e5m2, 14)}[fmt]
    v = np.moveaxis(np.asarray(x, np.float32).astype(ml_dtypes.bfloat16).astype(np.float64), axis, -1)
    blocks = v.reshape(v.shape[:-1] + (-1, 32))
    amax = np.abs(blocks).max(-1, keepdims=True)
    byte = np.maximum(np.where(amax > 0, np.frexp(amax)[1] - 1 + 127, 0) - down, 1)
    scale = np.exp2(byte - 127.0)
    codes = (blocks / scale).astype(np.float32).astype(dtype).astype(np.float64)
    return np.moveaxis((codes * scale).reshape(v.shape), -1, axis)


WIDE = False


def mx_kscale(k):
    if not WIDE:
        return np.ones(k)
    levels = np.array([10, -10, 5, -5, 0])
    if k % 512:
        return np.exp2(np.random.permutation(np.resize(levels, k // 32))).repeat(32)
    a = np.empty((k // 512, 16))
    for p in range(k // 512):
        a[p, :8] = np.random.permutation(np.resize(levels, 8))
        for g in range(8):
            far = levels[np.abs(levels - a[p, g]) >= 10]
            a[p, g + 8] = far[np.random.randint(len(far))]
    return np.exp2(a.ravel()).repeat(32)


def f64(x):
    return np.asarray(x).astype(np.float64)


def striped(idx):
    return np.tile(np.asarray(idx).reshape(-1, 16).T, (8, 1)).astype(np.uint16)


def unstriped(offs):
    return offs[:16].T.reshape(-1).astype(np.int64)


E2M1 = np.array([0.0, 0.5, 1.0, 1.5, 2.0, 3.0, 4.0, 6.0, -0.0, -0.5, -1.0, -1.5, -2.0, -3.0, -4.0, -6.0])


def pack_weight(w, fmt):
    k, n = w.shape
    w = f64(np.asarray(w, np.float32).astype(ml_dtypes.bfloat16)).reshape(k // 32, 32, n)
    amax = np.abs(w).max(1)
    if fmt == "e4m3":
        byte = np.frexp(amax)[1] - 1 + 127 - 7
    else:
        mant, ex = np.frexp(amax / 6.0)
        byte = np.where(mant > 0.5, ex, ex - 1) + 127
    byte = np.clip(np.where(amax > 0, byte, 1), 1, 254)
    scaled = (w * np.exp2(127.0 - byte)[:, None, :]).reshape(k, n).astype(np.float32)
    by_word = np.ascontiguousarray(scaled.reshape(k // 512, 128, 4, n).transpose(0, 1, 3, 2))
    if fmt == "e4m3":
        words = by_word.astype(ml_dtypes.float8_e4m3fn).view(np.uint8)
    else:
        c = by_word.astype(ml_dtypes.float4_e2m1fn).view(np.uint8) & 0xF
        words = (c[..., 0::2] | (c[..., 1::2] << 4)).reshape(k // 512, 128, 2 * n)
    return np.ascontiguousarray(words), np.ascontiguousarray(byte.astype(np.uint8).reshape(k // 512, 16, n))


def unpack_weight(words, scales, fmt):
    g, _, n = scales.shape
    words = np.ascontiguousarray(words).reshape(g, 128, n, -1)
    if fmt == "e4m3":
        vals = words.view(ml_dtypes.float8_e4m3fn).astype(np.float64)
    else:
        nib = np.empty((g, 128, n, 4), np.uint8)
        nib[..., 0::2] = words & 0xF
        nib[..., 1::2] = words >> 4
        vals = E2M1[nib]
    vals = vals * np.repeat(np.exp2(scales.astype(np.float64) - 127.0), 8, axis=1)[..., None]
    return vals.transpose(0, 1, 3, 2).reshape(g * 512, n)


def elu1(v):
    return np.maximum(v, 0.0) + np.exp(np.minimum(v, 0.0))


def sigmoid(v):
    return 1.0 / (1.0 + np.exp(-v))


D, T, I, Q, E, F = 512, 2048, 512, 128, 512, 512


def setup_inputs():
    n = np.random.standard_normal
    idx = np.random.permutation(T)[:I]
    fd = mx_kscale(D)
    fi = mx_kscale(I)
    ff = mx_kscale(F)
    ti = np.ones(T)
    ti[idx] = fi
    keysp = pack_weight(n((D, T)) / fd[:, None], "e4m3")
    return {
        "query": (n((D, Q)) * 0.4 / np.sqrt(D) * fd[:, None]).astype(np.float32),
        "keys_words": keysp[0],
        "keys_scales": keysp[1],
        "vals": (n((E, T)) / ti).astype(np.float32),
        "size": (np.random.uniform(0.5, 2.0, (1, I)) * fi).astype(np.float32),
        "mq": (n((F, Q))).astype(np.float32),
        "fsc": (np.random.uniform(0.5, 2.0, (F, 1)) * ff[:, None]).astype(np.float32),
        "state": (n((F, E)) * 1 / np.sqrt(F) / ff[:, None]).astype(np.float32),
        "den": (np.random.uniform(0.8, 1.2, (Q, 1))).astype(np.float32),
        "gb": (np.random.uniform(-1.5, 1.5, (Q, 1))).astype(np.float32),
        "offs": striped(idx),
    }


def reference(query, keys_words, keys_scales, vals, size, mq, fsc, state, den, gb, offs):
    idx = unstriped(offs)
    keysu = unpack_weight(keys_words, keys_scales, "e4m3")
    queryq = mxq(f64(query), 0, "e4m3")
    keysidxg = keysu[:, idx]
    a = queryq.T @ keysidxg
    p = np.exp(a - np.max(a, axis=1, keepdims=True))
    w = p * f64(size) / np.sum(p, axis=1, keepdims=True)
    wt = w.T
    vt = f64(vals)[:, idx].T
    wtq = mxq(wt, 0, "e4m3")
    vtq = mxq(vt, 0, "e4m3")
    lo = wtq.T @ vtq
    phi = elu1(f64(mq)) * f64(fsc)
    phiq = mxq(phi, 0, "e4m3")
    stateq = mxq(f64(state), 0, "e4m3")
    me = phiq.T @ stateq
    g = sigmoid(f64(gb))
    o = g * 0.1 * me / f64(den) + (1.0 - g) * lo
    return o

@@ -1,0 +1,213 @@
+from contextlib import ExitStack
+
+import concourse.mybir as mybir
+from concourse.masks import make_identity
+
+D, T, I, Q, E, F = 512, 2048, 512, 128, 512, 512
+FLOPS = 2 * Q * (D * I + I * E + F * E)
+
+F32 = mybir.dt.float32
+BF16 = mybir.dt.bfloat16
+I32 = mybir.dt.int32
+U32 = mybir.dt.uint32
+U16 = mybir.dt.uint16
+U8 = mybir.dt.uint8
+FP8X4 = mybir.dt.float8_e4m3fn_x4
+ACT = mybir.ActivationFunctionType
+ALU = mybir.AluOpType
+AX = mybir.AxisListType
+
+P = 128
+PACK = 4
+COLS = 128
+HALF = 256
+SPLIT = 160
+
+
+def interleaved_views(dst, src):
+    return (
+        dst.rearrange("p (c i t) -> p c t i", i=4, t=PACK),
+        src.rearrange("p t (c i) -> p c t i", i=4),
+    )
+
+
+def tile_attend_infini_kernel(tc, query, keys_words, keys_scales, vals, size, mq, fsc, state, den, gb, offs, out):
+    nc = tc.nc
+    with ExitStack() as ctx:
+        sb = ctx.enter_context(tc.tile_pool(name="sb", bufs=1))
+        ps = ctx.enter_context(tc.psum_pool(name="ps", bufs=1))
+
+        def quantize(values, name, slot=None):
+            width = values.shape[1] // PACK
+            codes = sb.tile([P, width], U32, name=name + "_codes", tag=slot or name + "_codes", align_bytes=64)
+            scales = sb.tile([P, width], U8, name=name + "_scales", align_bytes=64)
+            nc.vector.quantize_mx(out=codes[:].bitcast(FP8X4), scales=scales[:], in_=values)
+            return codes[:], scales[:]
+
+        def product(dst, rows, cols):
+            nc.tensor.matmul_mx(
+                out=dst, lhsT=rows[0].bitcast(FP8X4), lhsT_scale=rows[1],
+                rhs=cols[0].bitcast(FP8X4), rhs_scale=cols[1], start=True, stop=True,
+            )
+
+        def turn(values, name, turned):
+            words = values.bitcast(F32)
+            bank = ps.tile([P, 2, P], F32, name=name + "_bank", tag="turn", bufs=3)
+            for u in range(2):
+                nc.tensor.transpose(bank[:, u, :], words[:, u : I // 2 : 2], ident[:])
+            nc.scalar.copy(
+                out=turned.bitcast(F32).rearrange("p (c u) -> p c u", u=2),
+                in_=bank[:].rearrange("p u c -> p c u"),
+            )
+
+        key_bytes = sb.tile([P, T], U8, name="key_bytes", tag="slot_a", align_bytes=64)
+        nc.vector.memset(key_bytes[:, : T // 2].bitcast(I32), 0)
+        nc.gpsimd.memset(key_bytes[:, T // 2 :].bitcast(I32), 0)
+        offsets = sb.tile([P, I // 16], U16, name="offsets")
+        nc.sync.dma_start(offsets[:], offs)
+        gate_in = sb.tile([P, 1], F32, name="gate_in")
+        nc.scalar.dma_start(gate_in[:], gb)
+        size_cols = sb.tile([P, PACK], F32, name="size_cols")
+        nc.sync.dma_start(size_cols[:], size.rearrange("o (p t) -> (o p) t", t=PACK))
+        fsc_cols = sb.tile([P, PACK], F32, name="fsc_cols")
+        nc.sync.dma_start(fsc_cols[:], fsc.rearrange("(p t) o -> p (t o)", t=PACK))
+        den_col = sb.tile([P, 1], F32, name="den_col")
+        nc.sync.dma_start(den_col[:], den)
+        key_words = sb.tile([P, T], U32, name="key_words")
+        words_in = keys_words[0].rearrange("p n t -> p (n t)").bitcast(I32)
+        for h in range(2):
+            cols = slice(h * T // 2, (h + 1) * T // 2)
+            nc.sync.dma_start(key_words[:, cols].bitcast(I32), words_in[:, cols])
+        query_raw = sb.tile([P, PACK, Q], F32, name="query_raw")
+        nc.sync.dma_start(query_raw[:], query.rearrange("(p t) q -> p t q", t=PACK))
+        mq_raw = sb.tile([P, PACK, Q], F32, name="mq_raw")
+        nc.sync.dma_start(mq_raw[:], mq.rearrange("(p t) q -> p t q", t=PACK))
+        for quad in range(4):
+            nc.sync.dma_start(
+                key_bytes[32 * quad : 32 * quad + 4, :].bitcast(I32),
+                keys_scales[0, 4 * quad : 4 * quad + 4, :].bitcast(I32),
+            )
+        pools = []
+        for c in range(E // COLS):
+            pool_c = sb.tile([P, T], F32, name="vals%d" % c, tag="slot_f" if c == 3 else "vals%d" % c, align_bytes=64)
+            nc.sync.dma_start(pool_c[:], vals[c * COLS : (c + 1) * COLS, :])
+            pools.append(pool_c)
+        state_raw = [None, None]
+        for h in (1, 0):
+            state_raw[h] = sb.tile([P, PACK, HALF], F32, name="state%d" % h)
+            nc.sync.dma_start(
+                state_raw[h][:], state.rearrange("(p t) e -> p t e", t=PACK)[:, :, h * HALF : (h + 1) * HALF]
+            )
+
+        ident = sb.tile([P, P], F32, name="ident")
+        make_identity(nc, ident[:])
+
+        half_tanh = sb.tile([P, 1], F32, name="half_tanh")
+        nc.scalar.activation(half_tanh[:], gate_in[:], ACT.Tanh, scale=0.5)
+        local_share = sb.tile([P, 1], F32, name="local_share")
+        nc.scalar.activation(local_share[:], half_tanh[:], ACT.Copy, scale=-0.5, bias=0.5)
+        tenth_gate = sb.tile([P, 1], F32, name="tenth_gate")
+        nc.scalar.activation(tenth_gate[:], half_tanh[:], ACT.Copy, scale=0.05, bias=0.05)
+        inv_den = sb.tile([P, 1], F32, name="inv_den")
+        nc.vector.reciprocal(inv_den[:], den_col[:])
+        memory_share = sb.tile([P, 1], F32, name="memory_share")
+        nc.scalar.activation(memory_share[:], tenth_gate[:], ACT.Copy, scale=inv_den[:])
+
+        size_bank = ps.tile([P, PACK, P], F32, name="size_bank", tag="wide1")
+        for t in range(PACK):
+            nc.tensor.transpose(size_bank[:, t, :], size_cols[:, t : t + 1].to_broadcast([P, P]), ident[:])
+
+        picked_words = sb.tile([P, I], U32, name="picked_words", align_bytes=64)
+        nc.vector.tensor_copy(picked_words[:], key_words[:].indirect(offsets[:]))
+        picked_bytes = sb.tile([P, I], U8, name="picked_bytes", align_bytes=64)
+        nc.vector.tensor_copy(picked_bytes[:], key_bytes[:].indirect(offsets[:]))
+        query_bf = sb.tile([P, Q * PACK], BF16, name="query_bf", tag="slot_g", align_bytes=64)
+        dst, src = interleaved_views(query_bf[:], query_raw[:])
+        nc.scalar.copy(out=dst, in_=src)
+        query_mx = quantize(query_bf[:], "query", "slot_a")
+        scores = ps.tile([P, I], F32, name="scores", tag="wide0")
+        product(scores[:], query_mx, (picked_words[:], picked_bytes[:]))
+
+        below = sb.tile([P, PACK, Q], F32, name="below")
+        nc.scalar.activation(below[:], mq_raw[:], ACT.Relu, scale=-1.0)
+        decay = sb.tile([P, PACK, Q], F32, name="decay", tag="slot_b", align_bytes=64)
+        nc.scalar.activation(decay[:], below[:], ACT.Exp, scale=-1.0)
+        elu = sb.tile([P, PACK, Q], F32, name="elu", tag="slot_g", align_bytes=64)
+        nc.vector.scalar_tensor_tensor(elu[:], mq_raw[:], 0.0, decay[:], ALU.max, ALU.add)
+        vals_turned = [
+            sb.tile([P, HALF * PACK], BF16, name="vals_turned0", tag="slot_e", align_bytes=64),
+            sb.tile([P, HALF * PACK], BF16, name="vals_turned1", align_bytes=64),
+        ]
+        picked_slots = ["slot_b", "slot_b", "slot_d", "slot_e"]
+
+        def pick_and_turn(c):
+            picked = sb.tile([P, I], BF16, name="picked%d" % c, tag=picked_slots[c], align_bytes=64)
+            nc.vector.tensor_copy(picked[:], pools[c][:].indirect(offsets[:]))
+            k = c % 2
+            turn(picked[:], "vals%d" % c, vals_turned[c // 2][:, k * COLS * PACK : (k + 1) * COLS * PACK])
+
+        neg_max = sb.tile([P, 1], F32, name="neg_max")
+        nc.vector.tensor_reduce(neg_max[:], scores[:], AX.X, ALU.max, negate=True)
+        probs = sb.tile([P, I], F32, name="probs", tag="slot_d", align_bytes=64)
+        row_sum = sb.tile([P, 1], F32, name="row_sum")
+        nc.scalar.activation(probs[:], scores[:], ACT.Exp, bias=neg_max[:], accum_out=row_sum[:])
+        pick_and_turn(0)
+        phi_rows = sb.tile([P, PACK, Q], BF16, name="phi_rows")
+        for t in range(PACK):
+            nc.scalar.activation(phi_rows[:, t, :], elu[:, t, :], ACT.Copy, scale=fsc_cols[:, t : t + 1])
+        phi_bf = sb.tile([P, Q * PACK], BF16, name="phi_bf", align_bytes=64)
+        dst, src = interleaved_views(phi_bf[:], phi_rows[:])
+        nc.scalar.copy(out=dst, in_=src)
+
+        phi_mx = quantize(phi_bf[:], "phi")
+
+        pick_and_turn(1)
+
+        inv_sum = sb.tile([P, 1], F32, name="inv_sum")
+        nc.vector.reciprocal(inv_sum[:], row_sum[:])
+        weights = sb.tile([P, I], BF16, name="weights")
+        nc.vector.scalar_tensor_tensor(
+            weights[:].rearrange("q (s t) -> q s t", t=PACK),
+            probs[:].rearrange("q (s t) -> q s t", t=PACK),
+            inv_sum[:],
+            size_bank[:].rearrange("q t s -> q s t"),
+            ALU.mult, ALU.mult,
+        )
+        weights_turned = sb.tile([P, Q * PACK], BF16, name="weights_turned", align_bytes=64)
+        turn(weights[:], "weights", weights_turned[:])
+        pick_and_turn(2)
+        weights_mx = quantize(weights_turned[:], "weights")
+
+        def half_product(rows_mx, values, name, tag):
+            cols_mx = quantize(values, name)
+            bank = ps.tile([P, HALF], F32, name=name + "_bank", tag=tag)
+            product(bank[:], rows_mx, cols_mx)
+            return bank
+
+        def scaled(bank, share, name):
+            part = sb.tile([P, HALF], F32, name=name)
+            nc.scalar.activation(part[:], bank[:], ACT.Copy, scale=share[:])
+            return part
+
+        def mix_and_store(h, bank, share, part):
+            result = sb.tile([P, HALF], F32, name="result%d" % h)
+            nc.vector.scalar_tensor_tensor(result[:], bank[:], share[:], part[:], ALU.mult, ALU.add)
+            nc.sync.dma_start(out[:, h * HALF : (h + 1) * HALF], result[:])
+
+        local_low = scaled(half_product(weights_mx, vals_turned[0][:], "vals_low", "half0"), local_share, "local_low")
+        pick_and_turn(3)
+
+        state_high = sb.tile([P, HALF * PACK], BF16, name="state_high", tag="slot_f", align_bytes=64)
+        dst, src = interleaved_views(state_high[:], state_raw[1][:])
+        nc.vector.tensor_copy(out=dst, in_=src)
+        memory_high = scaled(half_product(phi_mx, state_high[:], "state_high", "wide0"), memory_share, "memory_high")
+
+        state_low = sb.tile([P, HALF * PACK], BF16, name="state_low", tag="slot_f", align_bytes=64)
+        dst, src = interleaved_views(state_low[:, : SPLIT * PACK], state_raw[0][:, :, :SPLIT])
+        nc.vector.tensor_copy(out=dst, in_=src)
+        dst, src = interleaved_views(state_low[:, SPLIT * PACK :], state_raw[0][:, :, SPLIT:])
+        nc.scalar.copy(out=dst, in_=src)
+        local_high_bank = half_product(weights_mx, vals_turned[1][:], "vals_high", "half1")
+        memory_low_bank = half_product(phi_mx, state_low[:], "state_low", "wide1")
+        mix_and_store(1, local_high_bank, local_share, memory_high)
+        mix_and_store(0, memory_low_bank, memory_share, local_low)

@@ -67,6 +67,8 @@ def tile_attend_infini_kernel(tc, query, keys_words, keys_scales, vals, size, mq
         nc.sync.dma_start(offsets[:], offs)
         gate_in = sb.tile([P, 1], F32, name="gate_in")
         nc.scalar.dma_start(gate_in[:], gb)
+        query_raw = sb.tile([P, PACK, Q], F32, name="query_raw")
+        nc.sync.dma_start(query_raw[:], query.rearrange("(p t) q -> p t q", t=PACK))
         size_cols = sb.tile([P, PACK], F32, name="size_cols")
         nc.sync.dma_start(size_cols[:], size.rearrange("o (p t) -> (o p) t", t=PACK))
         fsc_cols = sb.tile([P, PACK], F32, name="fsc_cols")
@@ -78,8 +80,6 @@ def tile_attend_infini_kernel(tc, query, keys_words, keys_scales, vals, size, mq
         for h in range(2):
             cols = slice(h * T // 2, (h + 1) * T // 2)
             nc.sync.dma_start(key_words[:, cols].bitcast(I32), words_in[:, cols])
-        query_raw = sb.tile([P, PACK, Q], F32, name="query_raw")
-        nc.sync.dma_start(query_raw[:], query.rearrange("(p t) q -> p t q", t=PACK))
         mq_raw = sb.tile([P, PACK, Q], F32, name="mq_raw")
         nc.sync.dma_start(mq_raw[:], mq.rearrange("(p t) q -> p t q", t=PACK))
         for quad in range(4):
@@ -87,17 +87,15 @@ def tile_attend_infini_kernel(tc, query, keys_words, keys_scales, vals, size, mq
                 key_bytes[32 * quad : 32 * quad + 4, :].bitcast(I32),
                 keys_scales[0, 4 * quad : 4 * quad + 4, :].bitcast(I32),
             )
-        pools = []
-        for c in range(E // COLS):
-            pool_c = sb.tile([P, T], F32, name="vals%d" % c, tag="slot_f" if c == 3 else "vals%d" % c, align_bytes=64)
-            nc.sync.dma_start(pool_c[:], vals[c * COLS : (c + 1) * COLS, :])
-            pools.append(pool_c)
-        state_raw = [None, None]
-        for h in (1, 0):
-            state_raw[h] = sb.tile([P, PACK, HALF], F32, name="state%d" % h)
-            nc.sync.dma_start(
-                state_raw[h][:], state.rearrange("(p t) e -> p t e", t=PACK)[:, :, h * HALF : (h + 1) * HALF]
-            )
+        state_rows = state.rearrange("(p t) e -> p t e", t=PACK)
+        pools = [sb.tile([P, T], F32, name="vals%d" % c, align_bytes=64) for c in range(E // COLS)]
+        state_high_raw = sb.tile([P, PACK, HALF], F32, name="state_high_raw", align_bytes=64)
+        state_low_raw = sb.tile([P, PACK, HALF], F32, name="state_low_raw", align_bytes=64)
+        for c in range(3):
+            nc.sync.dma_start(pools[c][:], vals[c * COLS : (c + 1) * COLS, :])
+        nc.sync.dma_start(state_high_raw[:], state_rows[:, :, HALF:])
+        nc.sync.dma_start(pools[3][:], vals[3 * COLS :, :])
+        nc.sync.dma_start(state_low_raw[:], state_rows[:, :, :HALF])
 
         ident = sb.tile([P, P], F32, name="ident")
         make_identity(nc, ident[:])
@@ -117,41 +115,34 @@ def tile_attend_infini_kernel(tc, query, keys_words, keys_scales, vals, size, mq
         for t in range(PACK):
             nc.tensor.transpose(size_bank[:, t, :], size_cols[:, t : t + 1].to_broadcast([P, P]), ident[:])
 
+        query_bf = sb.tile([P, Q * PACK], BF16, name="query_bf", align_bytes=64)
+        dst, src = interleaved_views(query_bf[:], query_raw[:])
+        nc.scalar.copy(out=dst, in_=src)
+        query_mx = quantize(query_bf[:], "query")
+
         picked_words = sb.tile([P, I], U32, name="picked_words", align_bytes=64)
         nc.vector.tensor_copy(picked_words[:], key_words[:].indirect(offsets[:]))
         picked_bytes = sb.tile([P, I], U8, name="picked_bytes", align_bytes=64)
         nc.vector.tensor_copy(picked_bytes[:], key_bytes[:].indirect(offsets[:]))
-        query_bf = sb.tile([P, Q * PACK], BF16, name="query_bf", tag="slot_g", align_bytes=64)
-        dst, src = interleaved_views(query_bf[:], query_raw[:])
-        nc.scalar.copy(out=dst, in_=src)
-        query_mx = quantize(query_bf[:], "query", "slot_a")
         scores = ps.tile([P, I], F32, name="scores", tag="wide0")
         product(scores[:], query_mx, (picked_words[:], picked_bytes[:]))
 
         below = sb.tile([P, PACK, Q], F32, name="below")
         nc.scalar.activation(below[:], mq_raw[:], ACT.Relu, scale=-1.0)
-        decay = sb.tile([P, PACK, Q], F32, name="decay", tag="slot_b", align_bytes=64)
+        decay = sb.tile([P, PACK, Q], F32, name="decay")
         nc.scalar.activation(decay[:], below[:], ACT.Exp, scale=-1.0)
-        elu = sb.tile([P, PACK, Q], F32, name="elu", tag="slot_g", align_bytes=64)
+        elu = sb.tile([P, PACK, Q], F32, name="elu", tag="slot_a", align_bytes=64)
         nc.vector.scalar_tensor_tensor(elu[:], mq_raw[:], 0.0, decay[:], ALU.max, ALU.add)
-        vals_turned = [
-            sb.tile([P, HALF * PACK], BF16, name="vals_turned0", tag="slot_e", align_bytes=64),
-            sb.tile([P, HALF * PACK], BF16, name="vals_turned1", align_bytes=64),
-        ]
-        picked_slots = ["slot_b", "slot_b", "slot_d", "slot_e"]
 
-        def pick_and_turn(c):
-            picked = sb.tile([P, I], BF16, name="picked%d" % c, tag=picked_slots[c], align_bytes=64)
-            nc.vector.tensor_copy(picked[:], pools[c][:].indirect(offsets[:]))
-            k = c % 2
-            turn(picked[:], "vals%d" % c, vals_turned[c // 2][:, k * COLS * PACK : (k + 1) * COLS * PACK])
+        def pick_and_turn(c, picked, turned):
+            nc.vector.tensor_copy(picked, pools[c][:].indirect(offsets[:]))
+            turn(picked, "vals%d" % c, turned)
 
-        neg_max = sb.tile([P, 1], F32, name="neg_max")
-        nc.vector.tensor_reduce(neg_max[:], scores[:], AX.X, ALU.max, negate=True)
-        probs = sb.tile([P, I], F32, name="probs", tag="slot_d", align_bytes=64)
-        row_sum = sb.tile([P, 1], F32, name="row_sum")
-        nc.scalar.activation(probs[:], scores[:], ACT.Exp, bias=neg_max[:], accum_out=row_sum[:])
-        pick_and_turn(0)
+        def mix_and_store(lo, bank, share, part):
+            result = sb.tile([P, HALF], F32, name="result%d" % lo)
+            nc.vector.scalar_tensor_tensor(result[:], bank[:], share[:], part, ALU.mult, ALU.add)
+            nc.sync.dma_start(out[:, lo : lo + HALF], result[:])
+
         phi_rows = sb.tile([P, PACK, Q], BF16, name="phi_rows")
         for t in range(PACK):
             nc.scalar.activation(phi_rows[:, t, :], elu[:, t, :], ACT.Copy, scale=fsc_cols[:, t : t + 1])
@@ -159,11 +150,18 @@ def tile_attend_infini_kernel(tc, query, keys_words, keys_scales, vals, size, mq
         dst, src = interleaved_views(phi_bf[:], phi_rows[:])
         nc.scalar.copy(out=dst, in_=src)
 
-        phi_mx = quantize(phi_bf[:], "phi")
+        neg_max = sb.tile([P, 1], F32, name="neg_max")
+        nc.vector.tensor_reduce(neg_max[:], scores[:], AX.X, ALU.max, negate=True)
+        probs = sb.tile([P, I], F32, name="probs")
+        row_sum = sb.tile([P, 1], F32, name="row_sum", tag="row_sum", align_bytes=64)
+        nc.scalar.activation(probs[:], scores[:], ACT.Exp, bias=neg_max[:], accum_out=row_sum[:])
 
-        pick_and_turn(1)
+        turned_low = sb.tile([P, HALF * PACK], BF16, name="turned_low", align_bytes=64)
+        picked = [sb.tile([P, I], BF16, name="picked%d" % c, align_bytes=64) for c in range(E // COLS)]
+        pick_and_turn(0, picked[0][:], turned_low[:, : COLS * PACK])
+        pick_and_turn(1, picked[1][:], turned_low[:, COLS * PACK :])
 
-        inv_sum = sb.tile([P, 1], F32, name="inv_sum")
+        inv_sum = sb.tile([P, 1], F32, name="inv_sum", tag="vals1", align_bytes=64)
         nc.vector.reciprocal(inv_sum[:], row_sum[:])
         weights = sb.tile([P, I], BF16, name="weights")
         nc.vector.scalar_tensor_tensor(
@@ -173,41 +171,41 @@ def tile_attend_infini_kernel(tc, query, keys_words, keys_scales, vals, size, mq
             size_bank[:].rearrange("q t s -> q s t"),
             ALU.mult, ALU.mult,
         )
-        weights_turned = sb.tile([P, Q * PACK], BF16, name="weights_turned", align_bytes=64)
-        turn(weights[:], "weights", weights_turned[:])
-        pick_and_turn(2)
-        weights_mx = quantize(weights_turned[:], "weights")
+        phi_mx = quantize(phi_bf[:], "phi", "row_sum")
 
-        def half_product(rows_mx, values, name, tag):
-            cols_mx = quantize(values, name)
-            bank = ps.tile([P, HALF], F32, name=name + "_bank", tag=tag)
-            product(bank[:], rows_mx, cols_mx)
-            return bank
-
-        def scaled(bank, share, name):
-            part = sb.tile([P, HALF], F32, name=name)
-            nc.scalar.activation(part[:], bank[:], ACT.Copy, scale=share[:])
-            return part
-
-        def mix_and_store(h, bank, share, part):
-            result = sb.tile([P, HALF], F32, name="result%d" % h)
-            nc.vector.scalar_tensor_tensor(result[:], bank[:], share[:], part[:], ALU.mult, ALU.add)
-            nc.sync.dma_start(out[:, h * HALF : (h + 1) * HALF], result[:])
-
-        local_low = scaled(half_product(weights_mx, vals_turned[0][:], "vals_low", "half0"), local_share, "local_low")
-        pick_and_turn(3)
-
-        state_high = sb.tile([P, HALF * PACK], BF16, name="state_high", tag="slot_f", align_bytes=64)
-        dst, src = interleaved_views(state_high[:], state_raw[1][:])
-        nc.vector.tensor_copy(out=dst, in_=src)
-        memory_high = scaled(half_product(phi_mx, state_high[:], "state_high", "wide0"), memory_share, "memory_high")
-
-        state_low = sb.tile([P, HALF * PACK], BF16, name="state_low", tag="slot_f", align_bytes=64)
-        dst, src = interleaved_views(state_low[:, : SPLIT * PACK], state_raw[0][:, :, :SPLIT])
-        nc.vector.tensor_copy(out=dst, in_=src)
-        dst, src = interleaved_views(state_low[:, SPLIT * PACK :], state_raw[0][:, :, SPLIT:])
+        state_high = sb.tile([P, HALF * PACK], BF16, name="state_high", tag="picked1", align_bytes=64)
+        dst, src = interleaved_views(state_high[:], state_high_raw[:])
         nc.scalar.copy(out=dst, in_=src)
-        local_high_bank = half_product(weights_mx, vals_turned[1][:], "vals_high", "half1")
-        memory_low_bank = half_product(phi_mx, state_low[:], "state_low", "wide1")
-        mix_and_store(1, local_high_bank, local_share, memory_high)
+
+        staged = sb.tile([P, 3 * HALF], F32, name="staged", tag="state_high_raw", align_bytes=64)
+        weights_turned = staged[:, :HALF].bitcast(BF16)
+        turned2 = staged[:, HALF : 2 * HALF].bitcast(BF16)
+        local_low = staged[:, 2 * HALF :]
+        turn(weights[:], "weights", weights_turned)
+        pick_and_turn(2, picked[2][:], turned2)
+        vals_low_mx = quantize(turned_low[:], "vals_low", "vals2")
+        state_high_mx = quantize(state_high[:], "state_high")
+        weights_mx = quantize(weights_turned, "weights")
+
+        memory_high_bank = ps.tile([P, HALF], F32, name="memory_high_bank", tag="wide0")
+        product(memory_high_bank[:], phi_mx, state_high_mx)
+        local_low_bank = ps.tile([P, HALF], F32, name="local_low_bank")
+        product(local_low_bank[:], weights_mx, vals_low_mx)
+        memory_high = sb.tile([P, HALF], F32, name="memory_high")
+        nc.scalar.activation(memory_high[:], memory_high_bank[:], ACT.Copy, scale=memory_share[:])
+        nc.scalar.activation(local_low, local_low_bank[:], ACT.Copy, scale=local_share[:])
+
+        turned3 = sb.tile([P, COLS * PACK], BF16, name="turned3", align_bytes=64)
+        pick_and_turn(3, picked[3][:], turned3[:])
+        state_low = sb.tile([P, HALF * PACK], BF16, name="state_low", tag="vals3", align_bytes=64)
+        dst, src = interleaved_views(state_low[:, : SPLIT * PACK], state_low_raw[:, :, :SPLIT])
+        nc.vector.tensor_copy(out=dst, in_=src)
+        dst, src = interleaved_views(state_low[:, SPLIT * PACK :], state_low_raw[:, :, SPLIT:])
+        nc.scalar.copy(out=dst, in_=src)
+        memory_low_bank = ps.tile([P, HALF], F32, name="memory_low_bank", tag="wide1")
+        product(memory_low_bank[:], phi_mx, quantize(state_low[:], "state_low"))
+        local_high_bank = ps.tile([P, HALF], F32, name="local_high_bank")
+        product(local_high_bank[:, :COLS], weights_mx, quantize(turned2, "vals2", "state_low_raw"))
+        product(local_high_bank[:, COLS:], weights_mx, quantize(turned3[:], "vals3"))
         mix_and_store(0, memory_low_bank, memory_share, local_low)
+        mix_and_store(HALF, local_high_bank, local_share, memory_high[:])

@@ -21,7 +21,7 @@ P = 128
 PACK = 4
 COLS = 128
 HALF = 256
-SPLIT = 160
+SPLIT = 176
 
 
 def interleaved_views(dst, src):
@@ -60,28 +60,31 @@ def tile_attend_infini_kernel(tc, query, keys_words, keys_scales, vals, size, mq
                 in_=bank[:].rearrange("p u c -> p c u"),
             )
 
-        key_bytes = sb.tile([P, T], U8, name="key_bytes", tag="slot_a", align_bytes=64)
+        key_bytes = sb.tile([P, T], U8, name="key_bytes")
         nc.vector.memset(key_bytes[:, : T // 2].bitcast(I32), 0)
         nc.gpsimd.memset(key_bytes[:, T // 2 :].bitcast(I32), 0)
+        ident = sb.tile([P, P], F32, name="ident")
+        make_identity(nc, ident[:])
         offsets = sb.tile([P, I // 16], U16, name="offsets")
         nc.sync.dma_start(offsets[:], offs)
         gate_in = sb.tile([P, 1], F32, name="gate_in")
         nc.scalar.dma_start(gate_in[:], gb)
-        query_raw = sb.tile([P, PACK, Q], F32, name="query_raw")
-        nc.sync.dma_start(query_raw[:], query.rearrange("(p t) q -> p t q", t=PACK))
         size_cols = sb.tile([P, PACK], F32, name="size_cols")
         nc.sync.dma_start(size_cols[:], size.rearrange("o (p t) -> (o p) t", t=PACK))
         fsc_cols = sb.tile([P, PACK], F32, name="fsc_cols")
-        nc.sync.dma_start(fsc_cols[:], fsc.rearrange("(p t) o -> p (t o)", t=PACK))
+        nc.gpsimd.dma_start(fsc_cols[:], fsc.rearrange("(p t) o -> p (t o)", t=PACK))
         den_col = sb.tile([P, 1], F32, name="den_col")
-        nc.sync.dma_start(den_col[:], den)
+        nc.gpsimd.dma_start(den_col[:], den)
+        mq_raw = sb.tile([P, PACK, Q], F32, name="mq_raw")
+        query_raw = sb.tile([P, PACK, Q], F32, name="query_raw")
+        for raw, rows in ((mq_raw, mq), (query_raw, query)):
+            for h in range(2):
+                nc.sync.dma_start(raw[:, 2 * h : 2 * h + 2, :], rows.rearrange("(p t) q -> p t q", t=PACK)[:, 2 * h : 2 * h + 2, :])
         key_words = sb.tile([P, T], U32, name="key_words")
         words_in = keys_words[0].rearrange("p n t -> p (n t)").bitcast(I32)
         for h in range(2):
             cols = slice(h * T // 2, (h + 1) * T // 2)
             nc.sync.dma_start(key_words[:, cols].bitcast(I32), words_in[:, cols])
-        mq_raw = sb.tile([P, PACK, Q], F32, name="mq_raw")
-        nc.sync.dma_start(mq_raw[:], mq.rearrange("(p t) q -> p t q", t=PACK))
         for quad in range(4):
             nc.sync.dma_start(
                 key_bytes[32 * quad : 32 * quad + 4, :].bitcast(I32),
@@ -90,15 +93,11 @@ def tile_attend_infini_kernel(tc, query, keys_words, keys_scales, vals, size, mq
         state_rows = state.rearrange("(p t) e -> p t e", t=PACK)
         pools = [sb.tile([P, T], F32, name="vals%d" % c, align_bytes=64) for c in range(E // COLS)]
         state_high_raw = sb.tile([P, PACK, HALF], F32, name="state_high_raw", align_bytes=64)
-        state_low_raw = sb.tile([P, PACK, HALF], F32, name="state_low_raw", align_bytes=64)
         for c in range(3):
             nc.sync.dma_start(pools[c][:], vals[c * COLS : (c + 1) * COLS, :])
         nc.sync.dma_start(state_high_raw[:], state_rows[:, :, HALF:])
         nc.sync.dma_start(pools[3][:], vals[3 * COLS :, :])
-        nc.sync.dma_start(state_low_raw[:], state_rows[:, :, :HALF])
 
-        ident = sb.tile([P, P], F32, name="ident")
-        make_identity(nc, ident[:])
 
         half_tanh = sb.tile([P, 1], F32, name="half_tanh")
         nc.scalar.activation(half_tanh[:], gate_in[:], ACT.Tanh, scale=0.5)
@@ -106,42 +105,21 @@ def tile_attend_infini_kernel(tc, query, keys_words, keys_scales, vals, size, mq
         nc.scalar.activation(local_share[:], half_tanh[:], ACT.Copy, scale=-0.5, bias=0.5)
         tenth_gate = sb.tile([P, 1], F32, name="tenth_gate")
         nc.scalar.activation(tenth_gate[:], half_tanh[:], ACT.Copy, scale=0.05, bias=0.05)
-        inv_den = sb.tile([P, 1], F32, name="inv_den")
-        nc.vector.reciprocal(inv_den[:], den_col[:])
-        memory_share = sb.tile([P, 1], F32, name="memory_share")
-        nc.scalar.activation(memory_share[:], tenth_gate[:], ACT.Copy, scale=inv_den[:])
 
         size_bank = ps.tile([P, PACK, P], F32, name="size_bank", tag="wide1")
         for t in range(PACK):
             nc.tensor.transpose(size_bank[:, t, :], size_cols[:, t : t + 1].to_broadcast([P, P]), ident[:])
 
+        below = sb.tile([P, PACK, Q], F32, name="below")
+        nc.scalar.activation(below[:], mq_raw[:], ACT.Relu, scale=-1.0)
+        decay = sb.tile([P, PACK, Q], F32, name="decay", align_bytes=64)
+        nc.scalar.activation(decay[:], below[:], ACT.Exp, scale=-1.0)
         query_bf = sb.tile([P, Q * PACK], BF16, name="query_bf", align_bytes=64)
         dst, src = interleaved_views(query_bf[:], query_raw[:])
         nc.scalar.copy(out=dst, in_=src)
         query_mx = quantize(query_bf[:], "query")
-
-        picked_words = sb.tile([P, I], U32, name="picked_words", align_bytes=64)
-        nc.vector.tensor_copy(picked_words[:], key_words[:].indirect(offsets[:]))
-        picked_bytes = sb.tile([P, I], U8, name="picked_bytes", align_bytes=64)
-        nc.vector.tensor_copy(picked_bytes[:], key_bytes[:].indirect(offsets[:]))
-        scores = ps.tile([P, I], F32, name="scores", tag="wide0")
-        product(scores[:], query_mx, (picked_words[:], picked_bytes[:]))
-
-        below = sb.tile([P, PACK, Q], F32, name="below")
-        nc.scalar.activation(below[:], mq_raw[:], ACT.Relu, scale=-1.0)
-        decay = sb.tile([P, PACK, Q], F32, name="decay")
-        nc.scalar.activation(decay[:], below[:], ACT.Exp, scale=-1.0)
-        elu = sb.tile([P, PACK, Q], F32, name="elu", tag="slot_a", align_bytes=64)
+        elu = sb.tile([P, PACK, Q], F32, name="elu")
         nc.vector.scalar_tensor_tensor(elu[:], mq_raw[:], 0.0, decay[:], ALU.max, ALU.add)
-
-        def pick_and_turn(c, picked, turned):
-            nc.vector.tensor_copy(picked, pools[c][:].indirect(offsets[:]))
-            turn(picked, "vals%d" % c, turned)
-
-        def mix_and_store(lo, bank, share, part):
-            result = sb.tile([P, HALF], F32, name="result%d" % lo)
-            nc.vector.scalar_tensor_tensor(result[:], bank[:], share[:], part, ALU.mult, ALU.add)
-            nc.sync.dma_start(out[:, lo : lo + HALF], result[:])
 
         phi_rows = sb.tile([P, PACK, Q], BF16, name="phi_rows")
         for t in range(PACK):
@@ -149,6 +127,23 @@ def tile_attend_infini_kernel(tc, query, keys_words, keys_scales, vals, size, mq
         phi_bf = sb.tile([P, Q * PACK], BF16, name="phi_bf", align_bytes=64)
         dst, src = interleaved_views(phi_bf[:], phi_rows[:])
         nc.scalar.copy(out=dst, in_=src)
+
+        picked_words = sb.tile([P, I], U32, name="picked_words", tag="decay", align_bytes=64)
+        nc.vector.tensor_copy(picked_words[:], key_words[:].indirect(offsets[:]))
+        picked_bytes = sb.tile([P, I], U8, name="picked_bytes", align_bytes=64)
+        nc.vector.tensor_copy(picked_bytes[:], key_bytes[:].indirect(offsets[:]))
+        scores = ps.tile([P, I], F32, name="scores", tag="wide0")
+        product(scores[:], query_mx, (picked_words[:], picked_bytes[:]))
+
+        def pick_and_turn(c, picked, turned):
+            nc.vector.tensor_copy(picked, pools[c][:].indirect(offsets[:]))
+            turn(picked, "vals%d" % c, turned)
+
+        def mix_and_store(lo, bank, share, part):
+            width = bank.shape[1]
+            result = sb.tile([P, width], F32, name="result%d" % lo)
+            nc.vector.scalar_tensor_tensor(result[:], bank[:], share[:], part, ALU.mult, ALU.add)
+            nc.sync.dma_start(out[:, lo : lo + width], result[:])
 
         neg_max = sb.tile([P, 1], F32, name="neg_max")
         nc.vector.tensor_reduce(neg_max[:], scores[:], AX.X, ALU.max, negate=True)
@@ -163,7 +158,7 @@ def tile_attend_infini_kernel(tc, query, keys_words, keys_scales, vals, size, mq
 
         inv_sum = sb.tile([P, 1], F32, name="inv_sum", tag="vals1", align_bytes=64)
         nc.vector.reciprocal(inv_sum[:], row_sum[:])
-        weights = sb.tile([P, I], BF16, name="weights")
+        weights = sb.tile([P, I], BF16, name="weights", align_bytes=64)
         nc.vector.scalar_tensor_tensor(
             weights[:].rearrange("q (s t) -> q s t", t=PACK),
             probs[:].rearrange("q (s t) -> q s t", t=PACK),
@@ -172,20 +167,27 @@ def tile_attend_infini_kernel(tc, query, keys_words, keys_scales, vals, size, mq
             ALU.mult, ALU.mult,
         )
         phi_mx = quantize(phi_bf[:], "phi", "row_sum")
+        weights_turned = sb.tile([P, Q * PACK], BF16, name="weights_turned", align_bytes=64)
+        turn(weights[:], "weights", weights_turned[:])
+        state_low_raw = sb.tile([P, PACK, HALF], F32, name="state_low_raw", tag="vals1", align_bytes=64)
+        nc.sync.dma_start(state_low_raw[:], state_rows[:, :, :HALF])
+
+        inv_den = sb.tile([P, 1], F32, name="inv_den", tag="picked1", align_bytes=64)
+        nc.vector.reciprocal(inv_den[:], den_col[:])
+        memory_share = sb.tile([P, 1], F32, name="memory_share")
+        nc.scalar.activation(memory_share[:], tenth_gate[:], ACT.Copy, scale=inv_den[:])
 
         state_high = sb.tile([P, HALF * PACK], BF16, name="state_high", tag="picked1", align_bytes=64)
         dst, src = interleaved_views(state_high[:], state_high_raw[:])
         nc.scalar.copy(out=dst, in_=src)
 
-        staged = sb.tile([P, 3 * HALF], F32, name="staged", tag="state_high_raw", align_bytes=64)
-        weights_turned = staged[:, :HALF].bitcast(BF16)
-        turned2 = staged[:, HALF : 2 * HALF].bitcast(BF16)
-        local_low = staged[:, 2 * HALF :]
-        turn(weights[:], "weights", weights_turned)
+        staged = sb.tile([P, 2 * HALF], F32, name="staged", tag="state_high_raw", align_bytes=64)
+        turned2 = staged[:, :HALF].bitcast(BF16)
+        local_low = staged[:, HALF:]
         pick_and_turn(2, picked[2][:], turned2)
         vals_low_mx = quantize(turned_low[:], "vals_low", "vals2")
+        weights_mx = quantize(weights_turned[:], "weights", "turned_low")
         state_high_mx = quantize(state_high[:], "state_high")
-        weights_mx = quantize(weights_turned, "weights")
 
         memory_high_bank = ps.tile([P, HALF], F32, name="memory_high_bank", tag="wide0")
         product(memory_high_bank[:], phi_mx, state_high_mx)
@@ -197,15 +199,17 @@ def tile_attend_infini_kernel(tc, query, keys_words, keys_scales, vals, size, mq
 
         turned3 = sb.tile([P, COLS * PACK], BF16, name="turned3", align_bytes=64)
         pick_and_turn(3, picked[3][:], turned3[:])
-        state_low = sb.tile([P, HALF * PACK], BF16, name="state_low", tag="vals3", align_bytes=64)
+        state_low = sb.tile([P, HALF * PACK], BF16, name="state_low", align_bytes=64)
         dst, src = interleaved_views(state_low[:, : SPLIT * PACK], state_low_raw[:, :, :SPLIT])
         nc.vector.tensor_copy(out=dst, in_=src)
         dst, src = interleaved_views(state_low[:, SPLIT * PACK :], state_low_raw[:, :, SPLIT:])
         nc.scalar.copy(out=dst, in_=src)
+        local2_bank = ps.tile([P, COLS], F32, name="local2_bank")
+        product(local2_bank[:], weights_mx, quantize(turned2, "vals2", "vals3"))
         memory_low_bank = ps.tile([P, HALF], F32, name="memory_low_bank", tag="wide1")
         product(memory_low_bank[:], phi_mx, quantize(state_low[:], "state_low"))
-        local_high_bank = ps.tile([P, HALF], F32, name="local_high_bank")
-        product(local_high_bank[:, :COLS], weights_mx, quantize(turned2, "vals2", "state_low_raw"))
-        product(local_high_bank[:, COLS:], weights_mx, quantize(turned3[:], "vals3"))
+        mix_and_store(HALF, local2_bank, local_share, memory_high[:, :COLS])
+        local3_bank = ps.tile([P, COLS], F32, name="local3_bank")
+        product(local3_bank[:], weights_mx, quantize(turned3[:], "vals3"))
         mix_and_store(0, memory_low_bank, memory_share, local_low)
-        mix_and_store(HALF, local_high_bank, local_share, memory_high[:])
+        mix_and_store(HALF + COLS, local3_bank, local_share, memory_high[:, COLS:])

@@ -60,11 +60,9 @@ def tile_attend_infini_kernel(tc, query, keys_words, keys_scales, vals, size, mq
                 in_=bank[:].rearrange("p u c -> p c u"),
             )
 
-        key_bytes = sb.tile([P, T], U8, name="key_bytes")
+        key_bytes = sb.tile([P, T], U8, name="key_bytes", tag="slot_a", align_bytes=64)
         nc.vector.memset(key_bytes[:, : T // 2].bitcast(I32), 0)
         nc.gpsimd.memset(key_bytes[:, T // 2 :].bitcast(I32), 0)
-        ident = sb.tile([P, P], F32, name="ident")
-        make_identity(nc, ident[:])
         offsets = sb.tile([P, I // 16], U16, name="offsets")
         nc.sync.dma_start(offsets[:], offs)
         gate_in = sb.tile([P, 1], F32, name="gate_in")
@@ -72,19 +70,18 @@ def tile_attend_infini_kernel(tc, query, keys_words, keys_scales, vals, size, mq
         size_cols = sb.tile([P, PACK], F32, name="size_cols")
         nc.sync.dma_start(size_cols[:], size.rearrange("o (p t) -> (o p) t", t=PACK))
         fsc_cols = sb.tile([P, PACK], F32, name="fsc_cols")
-        nc.gpsimd.dma_start(fsc_cols[:], fsc.rearrange("(p t) o -> p (t o)", t=PACK))
+        nc.sync.dma_start(fsc_cols[:], fsc.rearrange("(p t) o -> p (t o)", t=PACK))
         den_col = sb.tile([P, 1], F32, name="den_col")
-        nc.gpsimd.dma_start(den_col[:], den)
-        mq_raw = sb.tile([P, PACK, Q], F32, name="mq_raw")
-        query_raw = sb.tile([P, PACK, Q], F32, name="query_raw")
-        for raw, rows in ((mq_raw, mq), (query_raw, query)):
-            for h in range(2):
-                nc.sync.dma_start(raw[:, 2 * h : 2 * h + 2, :], rows.rearrange("(p t) q -> p t q", t=PACK)[:, 2 * h : 2 * h + 2, :])
+        nc.sync.dma_start(den_col[:], den)
         key_words = sb.tile([P, T], U32, name="key_words")
         words_in = keys_words[0].rearrange("p n t -> p (n t)").bitcast(I32)
         for h in range(2):
             cols = slice(h * T // 2, (h + 1) * T // 2)
             nc.sync.dma_start(key_words[:, cols].bitcast(I32), words_in[:, cols])
+        query_raw = sb.tile([P, PACK, Q], F32, name="query_raw")
+        nc.sync.dma_start(query_raw[:], query.rearrange("(p t) q -> p t q", t=PACK))
+        mq_raw = sb.tile([P, PACK, Q], F32, name="mq_raw")
+        nc.sync.dma_start(mq_raw[:], mq.rearrange("(p t) q -> p t q", t=PACK))
         for quad in range(4):
             nc.sync.dma_start(
                 key_bytes[32 * quad : 32 * quad + 4, :].bitcast(I32),
@@ -98,6 +95,8 @@ def tile_attend_infini_kernel(tc, query, keys_words, keys_scales, vals, size, mq
         nc.sync.dma_start(state_high_raw[:], state_rows[:, :, HALF:])
         nc.sync.dma_start(pools[3][:], vals[3 * COLS :, :])
 
+        ident = sb.tile([P, P], F32, name="ident")
+        make_identity(nc, ident[:])
 
         half_tanh = sb.tile([P, 1], F32, name="half_tanh")
         nc.scalar.activation(half_tanh[:], gate_in[:], ACT.Tanh, scale=0.5)
@@ -105,21 +104,42 @@ def tile_attend_infini_kernel(tc, query, keys_words, keys_scales, vals, size, mq
         nc.scalar.activation(local_share[:], half_tanh[:], ACT.Copy, scale=-0.5, bias=0.5)
         tenth_gate = sb.tile([P, 1], F32, name="tenth_gate")
         nc.scalar.activation(tenth_gate[:], half_tanh[:], ACT.Copy, scale=0.05, bias=0.05)
+        inv_den = sb.tile([P, 1], F32, name="inv_den")
+        nc.vector.reciprocal(inv_den[:], den_col[:])
+        memory_share = sb.tile([P, 1], F32, name="memory_share")
+        nc.scalar.activation(memory_share[:], tenth_gate[:], ACT.Copy, scale=inv_den[:])
 
         size_bank = ps.tile([P, PACK, P], F32, name="size_bank", tag="wide1")
         for t in range(PACK):
             nc.tensor.transpose(size_bank[:, t, :], size_cols[:, t : t + 1].to_broadcast([P, P]), ident[:])
 
-        below = sb.tile([P, PACK, Q], F32, name="below")
-        nc.scalar.activation(below[:], mq_raw[:], ACT.Relu, scale=-1.0)
-        decay = sb.tile([P, PACK, Q], F32, name="decay", align_bytes=64)
-        nc.scalar.activation(decay[:], below[:], ACT.Exp, scale=-1.0)
+        picked_words = sb.tile([P, I], U32, name="picked_words", align_bytes=64)
+        nc.vector.tensor_copy(picked_words[:], key_words[:].indirect(offsets[:]))
         query_bf = sb.tile([P, Q * PACK], BF16, name="query_bf", align_bytes=64)
         dst, src = interleaved_views(query_bf[:], query_raw[:])
         nc.scalar.copy(out=dst, in_=src)
         query_mx = quantize(query_bf[:], "query")
-        elu = sb.tile([P, PACK, Q], F32, name="elu")
+        picked_bytes = sb.tile([P, I], U8, name="picked_bytes", align_bytes=64)
+        nc.vector.tensor_copy(picked_bytes[:], key_bytes[:].indirect(offsets[:]))
+        scores = ps.tile([P, I], F32, name="scores", tag="wide0")
+        product(scores[:], query_mx, (picked_words[:], picked_bytes[:]))
+
+        below = sb.tile([P, PACK, Q], F32, name="below")
+        nc.scalar.activation(below[:], mq_raw[:], ACT.Relu, scale=-1.0)
+        decay = sb.tile([P, PACK, Q], F32, name="decay")
+        nc.scalar.activation(decay[:], below[:], ACT.Exp, scale=-1.0)
+        elu = sb.tile([P, PACK, Q], F32, name="elu", tag="slot_a", align_bytes=64)
         nc.vector.scalar_tensor_tensor(elu[:], mq_raw[:], 0.0, decay[:], ALU.max, ALU.add)
+
+        def pick_and_turn(c, picked, turned):
+            nc.vector.tensor_copy(picked, pools[c][:].indirect(offsets[:]))
+            turn(picked, "vals%d" % c, turned)
+
+        def mix_and_store(lo, bank, share, part, slot):
+            width = bank.shape[1]
+            result = sb.tile([P, width], F32, name="result%d" % lo, tag=slot, align_bytes=64)
+            nc.vector.scalar_tensor_tensor(result[:], bank[:], share[:], part, ALU.mult, ALU.add)
+            nc.sync.dma_start(out[:, lo : lo + width], result[:])
 
         phi_rows = sb.tile([P, PACK, Q], BF16, name="phi_rows")
         for t in range(PACK):
@@ -127,23 +147,6 @@ def tile_attend_infini_kernel(tc, query, keys_words, keys_scales, vals, size, mq
         phi_bf = sb.tile([P, Q * PACK], BF16, name="phi_bf", align_bytes=64)
         dst, src = interleaved_views(phi_bf[:], phi_rows[:])
         nc.scalar.copy(out=dst, in_=src)
-
-        picked_words = sb.tile([P, I], U32, name="picked_words", tag="decay", align_bytes=64)
-        nc.vector.tensor_copy(picked_words[:], key_words[:].indirect(offsets[:]))
-        picked_bytes = sb.tile([P, I], U8, name="picked_bytes", align_bytes=64)
-        nc.vector.tensor_copy(picked_bytes[:], key_bytes[:].indirect(offsets[:]))
-        scores = ps.tile([P, I], F32, name="scores", tag="wide0")
-        product(scores[:], query_mx, (picked_words[:], picked_bytes[:]))
-
-        def pick_and_turn(c, picked, turned):
-            nc.vector.tensor_copy(picked, pools[c][:].indirect(offsets[:]))
-            turn(picked, "vals%d" % c, turned)
-
-        def mix_and_store(lo, bank, share, part):
-            width = bank.shape[1]
-            result = sb.tile([P, width], F32, name="result%d" % lo)
-            nc.vector.scalar_tensor_tensor(result[:], bank[:], share[:], part, ALU.mult, ALU.add)
-            nc.sync.dma_start(out[:, lo : lo + width], result[:])
 
         neg_max = sb.tile([P, 1], F32, name="neg_max")
         nc.vector.tensor_reduce(neg_max[:], scores[:], AX.X, ALU.max, negate=True)
@@ -158,7 +161,7 @@ def tile_attend_infini_kernel(tc, query, keys_words, keys_scales, vals, size, mq
 
         inv_sum = sb.tile([P, 1], F32, name="inv_sum", tag="vals1", align_bytes=64)
         nc.vector.reciprocal(inv_sum[:], row_sum[:])
-        weights = sb.tile([P, I], BF16, name="weights", align_bytes=64)
+        weights = sb.tile([P, I], BF16, name="weights")
         nc.vector.scalar_tensor_tensor(
             weights[:].rearrange("q (s t) -> q s t", t=PACK),
             probs[:].rearrange("q (s t) -> q s t", t=PACK),
@@ -167,27 +170,22 @@ def tile_attend_infini_kernel(tc, query, keys_words, keys_scales, vals, size, mq
             ALU.mult, ALU.mult,
         )
         phi_mx = quantize(phi_bf[:], "phi", "row_sum")
-        weights_turned = sb.tile([P, Q * PACK], BF16, name="weights_turned", align_bytes=64)
-        turn(weights[:], "weights", weights_turned[:])
         state_low_raw = sb.tile([P, PACK, HALF], F32, name="state_low_raw", tag="vals1", align_bytes=64)
         nc.sync.dma_start(state_low_raw[:], state_rows[:, :, :HALF])
-
-        inv_den = sb.tile([P, 1], F32, name="inv_den", tag="picked1", align_bytes=64)
-        nc.vector.reciprocal(inv_den[:], den_col[:])
-        memory_share = sb.tile([P, 1], F32, name="memory_share")
-        nc.scalar.activation(memory_share[:], tenth_gate[:], ACT.Copy, scale=inv_den[:])
 
         state_high = sb.tile([P, HALF * PACK], BF16, name="state_high", tag="picked1", align_bytes=64)
         dst, src = interleaved_views(state_high[:], state_high_raw[:])
         nc.scalar.copy(out=dst, in_=src)
 
-        staged = sb.tile([P, 2 * HALF], F32, name="staged", tag="state_high_raw", align_bytes=64)
-        turned2 = staged[:, :HALF].bitcast(BF16)
-        local_low = staged[:, HALF:]
+        staged = sb.tile([P, 3 * HALF], F32, name="staged", tag="state_high_raw", align_bytes=64)
+        weights_turned = staged[:, :HALF].bitcast(BF16)
+        turned2 = staged[:, HALF : 2 * HALF].bitcast(BF16)
+        local_low = staged[:, 2 * HALF :]
+        turn(weights[:], "weights", weights_turned)
         pick_and_turn(2, picked[2][:], turned2)
         vals_low_mx = quantize(turned_low[:], "vals_low", "vals2")
-        weights_mx = quantize(weights_turned[:], "weights", "turned_low")
         state_high_mx = quantize(state_high[:], "state_high")
+        weights_mx = quantize(weights_turned, "weights")
 
         memory_high_bank = ps.tile([P, HALF], F32, name="memory_high_bank", tag="wide0")
         product(memory_high_bank[:], phi_mx, state_high_mx)
@@ -208,8 +206,8 @@ def tile_attend_infini_kernel(tc, query, keys_words, keys_scales, vals, size, mq
         product(local2_bank[:], weights_mx, quantize(turned2, "vals2", "vals3"))
         memory_low_bank = ps.tile([P, HALF], F32, name="memory_low_bank", tag="wide1")
         product(memory_low_bank[:], phi_mx, quantize(state_low[:], "state_low"))
-        mix_and_store(HALF, local2_bank, local_share, memory_high[:, :COLS])
         local3_bank = ps.tile([P, COLS], F32, name="local3_bank")
         product(local3_bank[:], weights_mx, quantize(turned3[:], "vals3"))
-        mix_and_store(0, memory_low_bank, memory_share, local_low)
-        mix_and_store(HALF + COLS, local3_bank, local_share, memory_high[:, COLS:])
+        mix_and_store(HALF, local2_bank, local_share, memory_high[:, :COLS], "turned3")
+        mix_and_store(0, memory_low_bank, memory_share, local_low, "result_low")
+        mix_and_store(HALF + COLS, local3_bank, local_share, memory_high[:, COLS:], "result_last")

from contextlib import ExitStack

import concourse.mybir as mybir
from concourse.masks import make_identity

D, T, I, Q, E, F = 512, 2048, 512, 128, 512, 512
FLOPS = 2 * Q * (D * I + I * E + F * E)

F32 = mybir.dt.float32
BF16 = mybir.dt.bfloat16
I32 = mybir.dt.int32
U32 = mybir.dt.uint32
U16 = mybir.dt.uint16
U8 = mybir.dt.uint8
FP8X4 = mybir.dt.float8_e4m3fn_x4
ACT = mybir.ActivationFunctionType
ALU = mybir.AluOpType
AX = mybir.AxisListType

P = 128
PACK = 4
COLS = 128
HALF = 256
SPLIT = 176


def interleaved_views(dst, src):
    return (
        dst.rearrange("p (c i t) -> p c t i", i=4, t=PACK),
        src.rearrange("p t (c i) -> p c t i", i=4),
    )


def tile_attend_infini_kernel(tc, query, keys_words, keys_scales, vals, size, mq, fsc, state, den, gb, offs, out):
    nc = tc.nc
    with ExitStack() as ctx:
        sb = ctx.enter_context(tc.tile_pool(name="sb", bufs=1))
        ps = ctx.enter_context(tc.psum_pool(name="ps", bufs=1))

        def quantize(values, name, slot=None):
            width = values.shape[1] // PACK
            codes = sb.tile([P, width], U32, name=name + "_codes", tag=slot or name + "_codes", align_bytes=64)
            scales = sb.tile([P, width], U8, name=name + "_scales", align_bytes=64)
            nc.vector.quantize_mx(out=codes[:].bitcast(FP8X4), scales=scales[:], in_=values)
            return codes[:], scales[:]

        def product(dst, rows, cols):
            nc.tensor.matmul_mx(
                out=dst, lhsT=rows[0].bitcast(FP8X4), lhsT_scale=rows[1],
                rhs=cols[0].bitcast(FP8X4), rhs_scale=cols[1], start=True, stop=True,
            )

        def turn(values, name, turned):
            words = values.bitcast(F32)
            bank = ps.tile([P, 2, P], F32, name=name + "_bank", tag="turn", bufs=3)
            for u in range(2):
                nc.tensor.transpose(bank[:, u, :], words[:, u : I // 2 : 2], ident[:])
            nc.scalar.copy(
                out=turned.bitcast(F32).rearrange("p (c u) -> p c u", u=2),
                in_=bank[:].rearrange("p u c -> p c u"),
            )

        key_bytes = sb.tile([P, T], U8, name="key_bytes", tag="slot_a", align_bytes=64)
        nc.vector.memset(key_bytes[:, : T // 2].bitcast(I32), 0)
        nc.gpsimd.memset(key_bytes[:, T // 2 :].bitcast(I32), 0)
        offsets = sb.tile([P, I // 16], U16, name="offsets")
        nc.sync.dma_start(offsets[:], offs)
        gate_in = sb.tile([P, 1], F32, name="gate_in")
        nc.scalar.dma_start(gate_in[:], gb)
        size_cols = sb.tile([P, PACK], F32, name="size_cols")
        nc.sync.dma_start(size_cols[:], size.rearrange("o (p t) -> (o p) t", t=PACK))
        fsc_cols = sb.tile([P, PACK], F32, name="fsc_cols")
        nc.sync.dma_start(fsc_cols[:], fsc.rearrange("(p t) o -> p (t o)", t=PACK))
        den_col = sb.tile([P, 1], F32, name="den_col")
        nc.sync.dma_start(den_col[:], den)
        key_words = sb.tile([P, T], U32, name="key_words")
        words_in = keys_words[0].rearrange("p n t -> p (n t)").bitcast(I32)
        for h in range(2):
            cols = slice(h * T // 2, (h + 1) * T // 2)
            nc.sync.dma_start(key_words[:, cols].bitcast(I32), words_in[:, cols])
        query_raw = sb.tile([P, PACK, Q], F32, name="query_raw")
        nc.sync.dma_start(query_raw[:], query.rearrange("(p t) q -> p t q", t=PACK))
        mq_raw = sb.tile([P, PACK, Q], F32, name="mq_raw")
        nc.sync.dma_start(mq_raw[:], mq.rearrange("(p t) q -> p t q", t=PACK))
        for quad in range(4):
            nc.sync.dma_start(
                key_bytes[32 * quad : 32 * quad + 4, :].bitcast(I32),
                keys_scales[0, 4 * quad : 4 * quad + 4, :].bitcast(I32),
            )
        state_rows = state.rearrange("(p t) e -> p t e", t=PACK)
        pools = [sb.tile([P, T], F32, name="vals%d" % c, align_bytes=64) for c in range(E // COLS)]
        state_high_raw = sb.tile([P, PACK, HALF], F32, name="state_high_raw", align_bytes=64)
        for c in range(3):
            nc.sync.dma_start(pools[c][:], vals[c * COLS : (c + 1) * COLS, :])
        nc.sync.dma_start(state_high_raw[:], state_rows[:, :, HALF:])
        nc.sync.dma_start(pools[3][:], vals[3 * COLS :, :])

        ident = sb.tile([P, P], F32, name="ident")
        make_identity(nc, ident[:])

        half_tanh = sb.tile([P, 1], F32, name="half_tanh")
        nc.scalar.activation(half_tanh[:], gate_in[:], ACT.Tanh, scale=0.5)
        local_share = sb.tile([P, 1], F32, name="local_share")
        nc.scalar.activation(local_share[:], half_tanh[:], ACT.Copy, scale=-0.5, bias=0.5)
        tenth_gate = sb.tile([P, 1], F32, name="tenth_gate")
        nc.scalar.activation(tenth_gate[:], half_tanh[:], ACT.Copy, scale=0.05, bias=0.05)
        inv_den = sb.tile([P, 1], F32, name="inv_den")
        nc.vector.reciprocal(inv_den[:], den_col[:])
        memory_share = sb.tile([P, 1], F32, name="memory_share")
        nc.scalar.activation(memory_share[:], tenth_gate[:], ACT.Copy, scale=inv_den[:])

        size_bank = ps.tile([P, PACK, P], F32, name="size_bank", tag="wide1")
        for t in range(PACK):
            nc.tensor.transpose(size_bank[:, t, :], size_cols[:, t : t + 1].to_broadcast([P, P]), ident[:])

        picked_words = sb.tile([P, I], U32, name="picked_words", align_bytes=64)
        nc.vector.tensor_copy(picked_words[:], key_words[:].indirect(offsets[:]))
        query_bf = sb.tile([P, Q * PACK], BF16, name="query_bf", align_bytes=64)
        dst, src = interleaved_views(query_bf[:], query_raw[:])
        nc.scalar.copy(out=dst, in_=src)
        query_mx = quantize(query_bf[:], "query")
        picked_bytes = sb.tile([P, I], U8, name="picked_bytes", align_bytes=64)
        nc.vector.tensor_copy(picked_bytes[:], key_bytes[:].indirect(offsets[:]))
        scores = ps.tile([P, I], F32, name="scores", tag="wide0")
        product(scores[:], query_mx, (picked_words[:], picked_bytes[:]))

        below = sb.tile([P, PACK, Q], F32, name="below")
        nc.scalar.activation(below[:], mq_raw[:], ACT.Relu, scale=-1.0)
        decay = sb.tile([P, PACK, Q], F32, name="decay")
        nc.scalar.activation(decay[:], below[:], ACT.Exp, scale=-1.0)
        elu = sb.tile([P, PACK, Q], F32, name="elu", tag="slot_a", align_bytes=64)
        nc.vector.scalar_tensor_tensor(elu[:], mq_raw[:], 0.0, decay[:], ALU.max, ALU.add)

        def pick_and_turn(c, picked, turned):
            nc.vector.tensor_copy(picked, pools[c][:].indirect(offsets[:]))
            turn(picked, "vals%d" % c, turned)

        def mix_and_store(lo, bank, share, part, slot):
            width = bank.shape[1]
            result = sb.tile([P, width], F32, name="result%d" % lo, tag=slot, align_bytes=64)
            nc.vector.scalar_tensor_tensor(result[:], bank[:], share[:], part, ALU.mult, ALU.add)
            nc.sync.dma_start(out[:, lo : lo + width], result[:])

        phi_rows = sb.tile([P, PACK, Q], BF16, name="phi_rows")
        for t in range(PACK):
            nc.scalar.activation(phi_rows[:, t, :], elu[:, t, :], ACT.Copy, scale=fsc_cols[:, t : t + 1])
        phi_bf = sb.tile([P, Q * PACK], BF16, name="phi_bf", align_bytes=64)
        dst, src = interleaved_views(phi_bf[:], phi_rows[:])
        nc.scalar.copy(out=dst, in_=src)

        neg_max = sb.tile([P, 1], F32, name="neg_max")
        nc.vector.tensor_reduce(neg_max[:], scores[:], AX.X, ALU.max, negate=True)
        probs = sb.tile([P, I], F32, name="probs")
        row_sum = sb.tile([P, 1], F32, name="row_sum", tag="row_sum", align_bytes=64)
        nc.scalar.activation(probs[:], scores[:], ACT.Exp, bias=neg_max[:], accum_out=row_sum[:])

        turned_low = sb.tile([P, HALF * PACK], BF16, name="turned_low", align_bytes=64)
        picked = [sb.tile([P, I], BF16, name="picked%d" % c, align_bytes=64) for c in range(E // COLS)]
        pick_and_turn(0, picked[0][:], turned_low[:, : COLS * PACK])
        pick_and_turn(1, picked[1][:], turned_low[:, COLS * PACK :])

        inv_sum = sb.tile([P, 1], F32, name="inv_sum", tag="vals1", align_bytes=64)
        nc.vector.reciprocal(inv_sum[:], row_sum[:])
        weights = sb.tile([P, I], BF16, name="weights")
        nc.vector.scalar_tensor_tensor(
            weights[:].rearrange("q (s t) -> q s t", t=PACK),
            probs[:].rearrange("q (s t) -> q s t", t=PACK),
            inv_sum[:],
            size_bank[:].rearrange("q t s -> q s t"),
            ALU.mult, ALU.mult,
        )
        phi_mx = quantize(phi_bf[:], "phi", "row_sum")
        state_low_raw = sb.tile([P, PACK, HALF], F32, name="state_low_raw", tag="vals1", align_bytes=64)
        nc.sync.dma_start(state_low_raw[:], state_rows[:, :, :HALF])

        state_high = sb.tile([P, HALF * PACK], BF16, name="state_high", tag="picked1", align_bytes=64)
        dst, src = interleaved_views(state_high[:], state_high_raw[:])
        nc.scalar.copy(out=dst, in_=src)

        staged = sb.tile([P, 3 * HALF], F32, name="staged", tag="state_high_raw", align_bytes=64)
        weights_turned = staged[:, :HALF].bitcast(BF16)
        turned2 = staged[:, HALF : 2 * HALF].bitcast(BF16)
        local_low = staged[:, 2 * HALF :]
        turn(weights[:], "weights", weights_turned)
        pick_and_turn(2, picked[2][:], turned2)
        vals_low_mx = quantize(turned_low[:], "vals_low", "vals2")
        state_high_mx = quantize(state_high[:], "state_high")
        weights_mx = quantize(weights_turned, "weights")

        memory_high_bank = ps.tile([P, HALF], F32, name="memory_high_bank", tag="wide0")
        product(memory_high_bank[:], phi_mx, state_high_mx)
        local_low_bank = ps.tile([P, HALF], F32, name="local_low_bank")
        product(local_low_bank[:], weights_mx, vals_low_mx)
        memory_high = sb.tile([P, HALF], F32, name="memory_high")
        nc.scalar.activation(memory_high[:], memory_high_bank[:], ACT.Copy, scale=memory_share[:])
        nc.scalar.activation(local_low, local_low_bank[:], ACT.Copy, scale=local_share[:])

        turned3 = sb.tile([P, COLS * PACK], BF16, name="turned3", align_bytes=64)
        pick_and_turn(3, picked[3][:], turned3[:])
        state_low = sb.tile([P, HALF * PACK], BF16, name="state_low", align_bytes=64)
        dst, src = interleaved_views(state_low[:, : SPLIT * PACK], state_low_raw[:, :, :SPLIT])
        nc.vector.tensor_copy(out=dst, in_=src)
        dst, src = interleaved_views(state_low[:, SPLIT * PACK :], state_low_raw[:, :, SPLIT:])
        nc.scalar.copy(out=dst, in_=src)
        local2_bank = ps.tile([P, COLS], F32, name="local2_bank")
        product(local2_bank[:], weights_mx, quantize(turned2, "vals2", "vals3"))
        memory_low_bank = ps.tile([P, HALF], F32, name="memory_low_bank", tag="wide1")
        product(memory_low_bank[:], phi_mx, quantize(state_low[:], "state_low"))
        local3_bank = ps.tile([P, COLS], F32, name="local3_bank")
        product(local3_bank[:], weights_mx, quantize(turned3[:], "vals3"))
        mix_and_store(HALF, local2_bank, local_share, memory_high[:, :COLS], "turned3")
        mix_and_store(0, memory_low_bank, memory_share, local_low, "result_low")
        mix_and_store(HALF + COLS, local3_bank, local_share, memory_high[:, COLS:], "result_last")
